import numpy as np
import ml_dtypes


def mxq(x, axis, fmt="e4m3"):
    dtype, down = {"e4m3": (ml_dtypes.float8_e4m3fn, 7), "e5m2": (ml_dtypes.float8_e5m2, 14)}[fmt]
    v = np.moveaxis(np.asarray(x, np.float32).astype(ml_dtypes.bfloat16).astype(np.float64), axis, -1)
    blocks = v.reshape(v.shape[:-1] + (-1, 32))
    amax = np.abs(blocks).max(-1, keepdims=True)
    byte = np.maximum(np.where(amax > 0, np.frexp(amax)[1] - 1 + 127, 0) - down, 1)
    scale = np.exp2(byte - 127.0)
    codes = (blocks / scale).astype(np.float32).astype(dtype).astype(np.float64)
    return np.moveaxis((codes * scale).reshape(v.shape), -1, axis)


WIDE = False


def mx_kscale(k):
    if not WIDE:
        return np.ones(k)
    levels = np.array([10, -10, 5, -5, 0])
    if k % 512:
        return np.exp2(np.random.permutation(np.resize(levels, k // 32))).repeat(32)
    a = np.empty((k // 512, 16))
    for p in range(k // 512):
        a[p, :8] = np.random.permutation(np.resize(levels, 8))
        for g in range(8):
            far = levels[np.abs(levels - a[p, g]) >= 10]
            a[p, g + 8] = far[np.random.randint(len(far))]
    return np.exp2(a.ravel()).repeat(32)


def f64(x):
    return np.asarray(x).astype(np.float64)


def striped(idx):
    return np.tile(idx.reshape(-1, 16).T, (8, 1)).astype(np.uint16)


def unstriped(offs):
    return offs[:16].T.reshape(-1).astype(np.int64)


E2M1 = np.array([0.0, 0.5, 1.0, 1.5, 2.0, 3.0, 4.0, 6.0, -0.0, -0.5, -1.0, -1.5, -2.0, -3.0, -4.0, -6.0])


def pack_weight(w, fmt):
    k, n = w.shape
    w = f64(np.asarray(w, np.float32).astype(ml_dtypes.bfloat16)).reshape(k // 32, 32, n)
    amax = np.abs(w).max(1)
    if fmt == "e4m3":
        byte = np.frexp(amax)[1] - 1 + 127 - 7
    else:
        mant, ex = np.frexp(amax / 6.0)
        byte = np.where(mant > 0.5, ex, ex - 1) + 127
    byte = np.clip(np.where(amax > 0, byte, 1), 1, 254)
    scaled = (w * np.exp2(127.0 - byte)[:, None, :]).reshape(k, n).astype(np.float32)
    by_word = np.ascontiguousarray(scaled.reshape(k // 512, 128, 4, n).transpose(0, 1, 3, 2))
    if fmt == "e4m3":
        words = by_word.astype(ml_dtypes.float8_e4m3fn).view(np.uint8)
    else:
        c = by_word.astype(ml_dtypes.float4_e2m1fn).view(np.uint8) & 0xF
        words = (c[..., 0::2] | (c[..., 1::2] << 4)).reshape(k // 512, 128, 2 * n)
    return np.ascontiguousarray(words), np.ascontiguousarray(byte.astype(np.uint8).reshape(k // 512, 16, n))


def unpack_weight(words, scales, fmt):
    g, _, n = scales.shape
    words = np.ascontiguousarray(words).reshape(g, 128, n, -1)
    if fmt == "e4m3":
        vals = words.view(ml_dtypes.float8_e4m3fn).astype(np.float64)
    else:
        nib = np.empty((g, 128, n, 4), np.uint8)
        nib[..., 0::2] = words & 0xF
        nib[..., 1::2] = words >> 4
        vals = E2M1[nib]
    vals = vals * np.repeat(np.exp2(scales.astype(np.float64) - 127.0), 8, axis=1)[..., None]
    return vals.transpose(0, 1, 3, 2).reshape(g * 512, n)


def relu2(v):
    return np.maximum(v, 0.0) ** 2


K, T, E, C, N = 1536, 512, 8, 256, 128
TOP = 4


def by_expert(wq, xq):
    return np.concatenate([wq[e].T @ xq[:, e * C:(e + 1) * C] for e in range(E)], axis=1)


def setup_inputs():
    n = np.random.standard_normal
    s = mx_kscale(K)[:, None]
    deal = np.repeat(np.arange(E), C).reshape(TOP, T)[:, np.random.permutation(T)]
    deal = np.take_along_axis(deal, np.argsort(np.random.rand(TOP, T), axis=0), axis=0)
    for _ in range(8):
        s_, t_ = np.random.permutation(T).reshape(2, -1); r = np.random.randint(TOP, size=T // 2); x, y = deal[r, s_].copy(), deal[r, t_].copy()
        ok = ~((deal[:, s_] == y).any(0) | (deal[:, t_] == x).any(0)); deal[r[ok], s_[ok]] = y[ok]; deal[r[ok], t_[ok]] = x[ok]
    order = np.lexsort((np.random.rand(TOP * T), deal.reshape(-1)))
    slot_token = order % T; pos = np.empty(TOP * T, np.int64); pos[order] = np.arange(TOP * T); pos = pos.reshape(TOP, T)
    g = np.random.uniform(0.5, 1.5, (TOP, T)); g = g / g.sum(0)
    w = [pack_weight(m, "e2m1") for m in n((E, K, N)) / np.sqrt(K) / s[None]]
    return {
        "xT": (n((K, T)) * s).astype(np.float32),
        "w_words": np.stack([m[0] for m in w]),
        "w_scales": np.stack([m[1] for m in w]),
        "b": (0.3 * n((N, E))).astype(np.float32),
        "gate": np.stack([np.tile(r, (N, 1)) for r in g]).astype(np.float32),
        "offs": striped(slot_token),
        "pos1": striped(pos[0]),
        "pos2": striped(pos[1]),
        "pos3": striped(pos[2]),
        "pos4": striped(pos[3]),
    }


def reference(xT, w_words, w_scales, b, gate, offs, pos1, pos2, pos3, pos4):
    idx = unstriped(offs)
    w = np.stack([unpack_weight(w_words[e], w_scales[e], "e2m1") for e in range(E)])
    xq = mxq(f64(xT)[:, idx], 0, "e4m3")
    y = by_expert(w, xq)
    y = relu2(y + np.repeat(f64(b), C, axis=1))
    return sum(f64(gate[r]) * y[:, unstriped(p)] for r, p in enumerate((pos1, pos2, pos3, pos4)))

@@ -1,0 +1,205 @@
+from contextlib import ExitStack
+
+import concourse.mybir as mybir
+
+K, T, E, C, N = 1536, 512, 8, 256, 128
+TOP = 4
+SLOTS = E * C
+P = 128
+A = K // 512
+FLOPS = 2 * K * N * SLOTS
+
+F32 = mybir.dt.float32
+BF16 = mybir.dt.bfloat16
+I32 = mybir.dt.int32
+U32 = mybir.dt.uint32
+U16 = mybir.dt.uint16
+U8 = mybir.dt.uint8
+FP8X4 = mybir.dt.float8_e4m3fn_x4
+FP4X4 = mybir.dt.float4_e2m1fn_x4
+ACT = mybir.ActivationFunctionType
+ALU = mybir.AluOpType
+
+
+def tile_moe_tk_lin_relu2_kernel(
+    tc, xT, w_words, w_scales, b, gate, offs, pos1, pos2, pos3, pos4, out
+):
+    nc = tc.nc
+    with ExitStack() as ctx:
+        keep = ctx.enter_context(tc.tile_pool(name="keep", bufs=1))
+        ring = ctx.enter_context(tc.tile_pool(name="ring", bufs=3))
+        psum = ctx.enter_context(tc.psum_pool(name="psum", bufs=8))
+
+        offs_t = keep.tile([P, SLOTS // 16], U16, name="offs_t")
+        pos_t = [keep.tile([P, T // 16], U16, name=f"pos_t{r}") for r in range(TOP)]
+        x_raw = [keep.tile([P, 4, T], F32, name=f"x_raw{a}") for a in range(A)]
+        x_bf = [keep.tile([P, T, 4], BF16, name=f"x_bf{a}", align_bytes=64) for a in range(A)]
+        span = [3 * T, 2 * T, 2 * T]
+        codes = [keep.tile([P, span[a]], I32, name=f"codes{a}", align_bytes=64) for a in range(A)]
+        planes = keep.tile([P, 3 * T], U8, name="planes", align_bytes=64)
+        slot_codes = [keep.tile([P, SLOTS], I32, name=f"slot_codes{a}", align_bytes=64) for a in range(A)]
+        slot_planes = [keep.tile([P, SLOTS], U8, name=f"slot_planes{a}", align_bytes=64) for a in range(A)]
+        w_t = keep.tile([P, E * A, 2 * N], U8, name="w_t", align_bytes=64)
+        ws_t = keep.tile([P, E * A, N], U8, name="ws_t", align_bytes=64)
+        b_t = keep.tile([P, E], F32, name="b_t")
+        gate_t = keep.tile([P, TOP, T], F32, name="gate_t")
+        y_t = keep.tile([P, SLOTS], F32, name="y_t")
+        prod = [keep.tile([P, T], F32, name=f"prod{r}") for r in range(TOP)]
+        sums = [keep.tile([P, T], F32, name=f"sums{r}") for r in range(3)]
+        warm = keep.tile([P, 2], F32, name="warm")
+
+        def x_rows(a):
+            return xT[a * 512 : (a + 1) * 512, :].rearrange("(p j) t -> p j t", j=4)
+
+        half = T // 2
+        nc.sync.dma_start(out=x_raw[0][:, :, 0:half], in_=x_rows(0)[:, :, 0:half])
+        nc.sync.dma_start(out=x_raw[0][:, :, half:T], in_=x_rows(0)[:, :, half:T])
+        nc.sync.dma_start(offs_t[:], offs)
+        nc.sync.dma_start(out=x_raw[1][:], in_=x_rows(1))
+        nc.sync.dma_start(out=x_raw[2][:], in_=x_rows(2))
+
+        w_rows = w_words.rearrange("e a p c -> p (e a) c")
+        ws_rows = w_scales.rearrange("e a q n -> q (e a) n")
+        h_ea = E * A // 2
+        nc.vector.memset(ws_t[:].rearrange("p i n -> p (i n)").bitcast(I32), 0)
+        nc.sync.dma_start(out=w_t[:, 0:h_ea, :].bitcast(I32), in_=w_rows[:, 0:h_ea, :].bitcast(I32))
+        for q in range(4):
+            nc.sync.dma_start(
+                out=ws_t[32 * q : 32 * q + 4, :, :].bitcast(I32),
+                in_=ws_rows[4 * q : 4 * q + 4, :, :].bitcast(I32),
+            )
+        nc.sync.dma_start(out=w_t[:, h_ea:, :].bitcast(I32), in_=w_rows[:, h_ea:, :].bitcast(I32))
+        nc.sync.dma_start(out=b_t[:], in_=b)
+        for r, pos in enumerate((pos1, pos2, pos3, pos4)):
+            nc.sync.dma_start(pos_t[r][:], pos)
+        nc.sync.dma_start(out=gate_t[:], in_=gate.rearrange("r p t -> p r t"))
+
+        nc.vector.memset(warm[:, 0:1], 0.0)
+        nc.scalar.activation(warm[:, 1:2], warm[:, 0:1], ACT.Relu)
+        nc.vector.memset(codes[0][:, T:], 0)
+        nc.vector.memset(codes[1][:, T:], 0)
+        nc.vector.memset(codes[2][:, T:], 0)
+        nc.vector.memset(planes[:].bitcast(I32), 0)
+        for a in (1, 2):
+            nc.gpsimd.memset(slot_planes[a][:].bitcast(I32), 0)
+
+        def interleave(copy, a, t0, t1):
+            copy(x_bf[a][:, t0:t1, :], x_raw[a][:, :, t0:t1].rearrange("p j t -> p t j"))
+
+        def quantise(a, t0, t1):
+            nc.vector.quantize_mx(
+                out=codes[a][:, t0:t1].bitcast(FP8X4),
+                scales=planes[4 * a : P, t0:t1],
+                in_=x_bf[a][:, t0:t1, :].rearrange("p t j -> p (t j)"),
+            )
+
+        def gather_words(a, s0, s1):
+            nc.vector.tensor_copy(
+                slot_codes[a][:, s0:s1].bitcast(U32),
+                codes[a][:].bitcast(U32).indirect(offs_t[:, s0 // 16 : s1 // 16]),
+            )
+
+        def gather_bytes(s0, s1):
+            nc.vector.tensor_copy(slot_planes[0][:, s0:s1], planes[:].indirect(offs_t[:, s0 // 16 : s1 // 16]))
+            for a in (1, 2):
+                nc.sync.dma_start(
+                    out=slot_planes[a][0:100, s0:s1].bitcast(I32),
+                    in_=slot_planes[0][4 * a : 4 * a + 100, s0:s1].bitcast(I32),
+                )
+
+        acc = {}
+
+        def multiply(e, h, passes):
+            if passes[0] == 0:
+                acc[(e, h)] = psum.tile([P, 512], F32, name="acc")
+            cols = slice(e * C + h * N, e * C + h * N + N)
+            for a in passes:
+                nc.tensor.matmul_mx(
+                    out=acc[(e, h)][:, 0:N],
+                    lhsT=w_t[:, e * A + a, :].bitcast(FP4X4),
+                    lhsT_scale=ws_t[:, e * A + a, :],
+                    rhs=slot_codes[a][:, cols].bitcast(FP8X4),
+                    rhs_scale=slot_planes[a][:, cols],
+                    start=(a == 0),
+                    stop=(a == A - 1),
+                )
+
+        def finish(e):
+            rel = ring.tile([P, C], F32, name="rel")
+            for h in range(2):
+                nc.scalar.activation(rel[:, h * N : (h + 1) * N], acc[(e, h)][:, 0:N], ACT.Relu, bias=b_t[:, e : e + 1])
+            nc.scalar.activation(y_t[:, e * C : (e + 1) * C], rel[:], ACT.Square)
+
+        interleave(nc.vector.tensor_copy, 0, 0, 256)
+        interleave(nc.vector.tensor_copy, 0, 256, 384)
+        interleave(nc.scalar.copy, 0, 384, 512)
+        quantise(0, 0, 256)
+        quantise(0, 256, 512)
+        gather_words(0, 0, 1024)
+        interleave(nc.scalar.copy, 1, 0, 512)
+        gather_words(0, 1024, 2048)
+        quantise(1, 0, 512)
+        interleave(nc.scalar.copy, 2, 0, 512)
+        gather_words(1, 0, 512)
+        gather_words(1, 512, 1024)
+        quantise(2, 0, 512)
+        gather_bytes(0, 1024)
+        gather_bytes(1024, 2048)
+        gather_words(2, 0, 512)
+        for e in (0, 1):
+            for h in range(2):
+                multiply(e, h, (0, 1, 2))
+            finish(e)
+        gather_words(2, 512, 1024)
+        for e in (2, 3):
+            for h in range(2):
+                multiply(e, h, (0, 1, 2))
+            finish(e)
+        gather_words(1, 1024, 1536)
+        for e in (4, 5):
+            for h in range(2):
+                multiply(e, h, (0, 1))
+        gather_words(1, 1536, 2048)
+        for e in (6, 7):
+            for h in range(2):
+                multiply(e, h, (0, 1))
+        gather_words(2, 1024, 1536)
+        for e in (4, 5):
+            for h in range(2):
+                multiply(e, h, (2,))
+            finish(e)
+        gather_words(2, 1536, 1792)
+        for h in range(2):
+            multiply(6, h, (2,))
+        finish(6)
+        gather_words(2, 1792, 1920)
+        multiply(7, 0, (2,))
+        gather_words(2, 1920, 2048)
+        multiply(7, 1, (2,))
+        last = 7 * C
+        rel_a = keep.tile([P, N], F32, name="rel_a")
+        rel_b = keep.tile([P, N], F32, name="rel_b")
+        nc.scalar.activation(rel_a[:], acc[(7, 0)][:, 0:N], ACT.Relu, bias=b_t[:, 7:8])
+        nc.scalar.activation(y_t[:, last : last + N], rel_a[:], ACT.Square)
+        nc.vector.tensor_scalar(rel_b[:], acc[(7, 1)][:, 0:N], b_t[:, 7:8], 0.0, ALU.add, ALU.max)
+        nc.vector.tensor_tensor(y_t[:, last + N : last + C], rel_b[:], rel_b[:], ALU.mult)
+
+        def fetch(r, t0, t1):
+            nc.vector.tensor_tensor(
+                prod[r][:, t0:t1],
+                y_t[:].indirect(pos_t[r][:, t0 // 16 : t1 // 16]),
+                gate_t[:, r, t0:t1],
+                ALU.mult,
+            )
+
+        fetch(0, 0, T)
+        fetch(1, 0, T)
+        fetch(2, 0, T)
+        nc.vector.tensor_tensor(sums[0][:], prod[0][:], prod[1][:], ALU.add)
+        fetch(3, 0, half)
+        nc.vector.tensor_tensor(sums[1][:], sums[0][:], prod[2][:], ALU.add)
+        fetch(3, half, T)
+        for t0 in (0, half):
+            cols = slice(t0, t0 + half)
+            nc.vector.tensor_tensor(sums[2][:, cols], sums[1][:, cols], prod[3][:, cols], ALU.add)
+            nc.sync.dma_start(out=out[:, cols], in_=sums[2][:, cols])

@@ -34,7 +34,7 @@ def tile_moe_tk_lin_relu2_kernel(
         pos_t = [keep.tile([P, T // 16], U16, name=f"pos_t{r}") for r in range(TOP)]
         x_raw = [keep.tile([P, 4, T], F32, name=f"x_raw{a}") for a in range(A)]
         x_bf = [keep.tile([P, T, 4], BF16, name=f"x_bf{a}", align_bytes=64) for a in range(A)]
-        span = [3 * T, 2 * T, 2 * T]
+        span = [3 * T, 3 * T, 2 * T]
         codes = [keep.tile([P, span[a]], I32, name=f"codes{a}", align_bytes=64) for a in range(A)]
         planes = keep.tile([P, 3 * T], U8, name="planes", align_bytes=64)
         slot_codes = [keep.tile([P, SLOTS], I32, name=f"slot_codes{a}", align_bytes=64) for a in range(A)]
@@ -60,15 +60,13 @@ def tile_moe_tk_lin_relu2_kernel(
 
         w_rows = w_words.rearrange("e a p c -> p (e a) c")
         ws_rows = w_scales.rearrange("e a q n -> q (e a) n")
-        h_ea = E * A // 2
         nc.vector.memset(ws_t[:].rearrange("p i n -> p (i n)").bitcast(I32), 0)
-        nc.sync.dma_start(out=w_t[:, 0:h_ea, :].bitcast(I32), in_=w_rows[:, 0:h_ea, :].bitcast(I32))
+        nc.sync.dma_start(out=w_t[:].bitcast(I32), in_=w_rows.bitcast(I32))
         for q in range(4):
             nc.sync.dma_start(
                 out=ws_t[32 * q : 32 * q + 4, :, :].bitcast(I32),
                 in_=ws_rows[4 * q : 4 * q + 4, :, :].bitcast(I32),
             )
-        nc.sync.dma_start(out=w_t[:, h_ea:, :].bitcast(I32), in_=w_rows[:, h_ea:, :].bitcast(I32))
         nc.sync.dma_start(out=b_t[:], in_=b)
         for r, pos in enumerate((pos1, pos2, pos3, pos4)):
             nc.sync.dma_start(pos_t[r][:], pos)
@@ -102,7 +100,7 @@ def tile_moe_tk_lin_relu2_kernel(
         def gather_bytes(s0, s1):
             nc.vector.tensor_copy(slot_planes[0][:, s0:s1], planes[:].indirect(offs_t[:, s0 // 16 : s1 // 16]))
             for a in (1, 2):
-                nc.sync.dma_start(
+                nc.scalar.dma_start(
                     out=slot_planes[a][0:100, s0:s1].bitcast(I32),
                     in_=slot_planes[0][4 * a : 4 * a + 100, s0:s1].bitcast(I32),
                 )
@@ -110,12 +108,10 @@ def tile_moe_tk_lin_relu2_kernel(
         acc = {}
 
         def multiply(e, h, passes):
-            if passes[0] == 0:
-                acc[(e, h)] = psum.tile([P, 512], F32, name="acc")
             cols = slice(e * C + h * N, e * C + h * N + N)
             for a in passes:
                 nc.tensor.matmul_mx(
-                    out=acc[(e, h)][:, 0:N],
+                    out=acc[(e, h)],
                     lhsT=w_t[:, e * A + a, :].bitcast(FP4X4),
                     lhsT_scale=ws_t[:, e * A + a, :],
                     rhs=slot_codes[a][:, cols].bitcast(FP8X4),
@@ -124,11 +120,18 @@ def tile_moe_tk_lin_relu2_kernel(
                     stop=(a == A - 1),
                 )
 
-        def finish(e):
-            rel = ring.tile([P, C], F32, name="rel")
-            for h in range(2):
-                nc.scalar.activation(rel[:, h * N : (h + 1) * N], acc[(e, h)][:, 0:N], ACT.Relu, bias=b_t[:, e : e + 1])
-            nc.scalar.activation(y_t[:, e * C : (e + 1) * C], rel[:], ACT.Square)
+        def experts(es):
+            banks, rels = {}, {}
+            for e in es:
+                banks[e] = psum.tile([P, 512], F32, name="acc")
+                for h in range(2):
+                    acc[(e, h)] = banks[e][:, h * N : (h + 1) * N]
+                    multiply(e, h, (0, 1, 2))
+            for e in es:
+                rels[e] = ring.tile([P, C], F32, name="rel")
+                nc.scalar.activation(rels[e][:], banks[e][:, 0:C], ACT.Relu, bias=b_t[:, e : e + 1])
+            for e in es:
+                nc.scalar.activation(y_t[:, e * C : (e + 1) * C], rels[e][:], ACT.Square)
 
         interleave(nc.vector.tensor_copy, 0, 0, 256)
         interleave(nc.vector.tensor_copy, 0, 256, 384)
@@ -140,49 +143,32 @@ def tile_moe_tk_lin_relu2_kernel(
         gather_words(0, 1024, 2048)
         quantise(1, 0, 512)
         interleave(nc.scalar.copy, 2, 0, 512)
-        gather_words(1, 0, 512)
-        gather_words(1, 512, 1024)
+        gather_words(1, 0, 1024)
         quantise(2, 0, 512)
         gather_bytes(0, 1024)
         gather_bytes(1024, 2048)
         gather_words(2, 0, 512)
-        for e in (0, 1):
-            for h in range(2):
-                multiply(e, h, (0, 1, 2))
-            finish(e)
+        experts((0, 1))
         gather_words(2, 512, 1024)
-        for e in (2, 3):
-            for h in range(2):
-                multiply(e, h, (0, 1, 2))
-            finish(e)
+        experts((2, 3))
         gather_words(1, 1024, 1536)
-        for e in (4, 5):
-            for h in range(2):
-                multiply(e, h, (0, 1))
-        gather_words(1, 1536, 2048)
-        for e in (6, 7):
-            for h in range(2):
-                multiply(e, h, (0, 1))
         gather_words(2, 1024, 1536)
-        for e in (4, 5):
-            for h in range(2):
-                multiply(e, h, (2,))
-            finish(e)
-        gather_words(2, 1536, 1792)
+        experts((4, 5))
+        gather_words(1, 1536, 2048)
         for h in range(2):
-            multiply(6, h, (2,))
-        finish(6)
-        gather_words(2, 1792, 1920)
-        multiply(7, 0, (2,))
-        gather_words(2, 1920, 2048)
-        multiply(7, 1, (2,))
+            acc[(7, h)] = psum.tile([P, 512], F32, name="acc")[:, 0:N]
+            multiply(7, h, (0, 1))
+        gather_words(2, 1536, 1792)
+        experts((6,))
+        gather_words(2, 1792, 2048)
         last = 7 * C
-        rel_a = keep.tile([P, N], F32, name="rel_a")
-        rel_b = keep.tile([P, N], F32, name="rel_b")
-        nc.scalar.activation(rel_a[:], acc[(7, 0)][:, 0:N], ACT.Relu, bias=b_t[:, 7:8])
-        nc.scalar.activation(y_t[:, last : last + N], rel_a[:], ACT.Square)
-        nc.vector.tensor_scalar(rel_b[:], acc[(7, 1)][:, 0:N], b_t[:, 7:8], 0.0, ALU.add, ALU.max)
-        nc.vector.tensor_tensor(y_t[:, last + N : last + C], rel_b[:], rel_b[:], ALU.mult)
+        rel7 = [keep.tile([P, N], F32, name=f"rel7_{h}") for h in range(2)]
+        for h in range(2):
+            multiply(7, h, (2,))
+        for h in range(2):
+            nc.vector.tensor_scalar(rel7[h][:], acc[(7, h)], b_t[:, 7:8], 0.0, ALU.add, ALU.max)
+        for h in range(2):
+            nc.vector.tensor_tensor(y_t[:, last + h * N : last + (h + 1) * N], rel7[h][:], rel7[h][:], ALU.mult)
 
         def fetch(r, t0, t1):
             nc.vector.tensor_tensor(
@@ -202,4 +188,4 @@ def tile_moe_tk_lin_relu2_kernel(
         for t0 in (0, half):
             cols = slice(t0, t0 + half)
             nc.vector.tensor_tensor(sums[2][:, cols], sums[1][:, cols], prod[3][:, cols], ALU.add)
-            nc.sync.dma_start(out=out[:, cols], in_=sums[2][:, cols])
+            (nc.sync if t0 == 0 else nc.scalar).dma_start(out=out[:, cols], in_=sums[2][:, cols])

@@ -33,11 +33,11 @@ def tile_moe_tk_lin_relu2_kernel(
         offs_t = keep.tile([P, SLOTS // 16], U16, name="offs_t")
         pos_t = [keep.tile([P, T // 16], U16, name=f"pos_t{r}") for r in range(TOP)]
         x_raw = [keep.tile([P, 4, T], F32, name=f"x_raw{a}") for a in range(A)]
-        x_bf = [keep.tile([P, T, 4], BF16, name=f"x_bf{a}", align_bytes=64) for a in range(A)]
-        span = [3 * T, 3 * T, 2 * T]
+        x_bf = [keep.tile([P, T, 4], BF16, name=f"x_bf{a}", tag=f"share{a}", align_bytes=64) for a in range(A)]
+        span = [1376, 1376, 704]
         codes = [keep.tile([P, span[a]], I32, name=f"codes{a}", align_bytes=64) for a in range(A)]
-        planes = keep.tile([P, 3 * T], U8, name="planes", align_bytes=64)
-        slot_codes = [keep.tile([P, SLOTS], I32, name=f"slot_codes{a}", align_bytes=64) for a in range(A)]
+        planes = keep.tile([P, 1376], U8, name="planes", align_bytes=64)
+        slot_codes = [[None, None], [None, None], [None, None]]
         slot_planes = [keep.tile([P, SLOTS], U8, name=f"slot_planes{a}", align_bytes=64) for a in range(A)]
         w_t = keep.tile([P, E * A, 2 * N], U8, name="w_t", align_bytes=64)
         ws_t = keep.tile([P, E * A, N], U8, name="ws_t", align_bytes=64)
@@ -60,7 +60,7 @@ def tile_moe_tk_lin_relu2_kernel(
 
         w_rows = w_words.rearrange("e a p c -> p (e a) c")
         ws_rows = w_scales.rearrange("e a q n -> q (e a) n")
-        nc.vector.memset(ws_t[:].rearrange("p i n -> p (i n)").bitcast(I32), 0)
+        nc.gpsimd.memset(ws_t[:].rearrange("p i n -> p (i n)").bitcast(I32), 0)
         nc.sync.dma_start(out=w_t[:].bitcast(I32), in_=w_rows.bitcast(I32))
         for q in range(4):
             nc.sync.dma_start(
@@ -74,10 +74,9 @@ def tile_moe_tk_lin_relu2_kernel(
 
         nc.vector.memset(warm[:, 0:1], 0.0)
         nc.scalar.activation(warm[:, 1:2], warm[:, 0:1], ACT.Relu)
-        nc.vector.memset(codes[0][:, T:], 0)
-        nc.vector.memset(codes[1][:, T:], 0)
-        nc.vector.memset(codes[2][:, T:], 0)
         nc.vector.memset(planes[:].bitcast(I32), 0)
+        for a in range(A):
+            nc.vector.memset(codes[a][:, T:], 0)
         for a in (1, 2):
             nc.gpsimd.memset(slot_planes[a][:].bitcast(I32), 0)
 
@@ -92,18 +91,23 @@ def tile_moe_tk_lin_relu2_kernel(
             )
 
         def gather_words(a, s0, s1):
+            i = s0 // 1024
+            if slot_codes[a][i] is None:
+                tag = "share2" if (a, i) == (1, 1) else f"slot_codes{a}_{i}"
+                slot_codes[a][i] = keep.tile([P, 1024], I32, name=f"slot_codes{a}_{i}", tag=tag, align_bytes=64)
             nc.vector.tensor_copy(
-                slot_codes[a][:, s0:s1].bitcast(U32),
+                slot_codes[a][i][:, s0 - 1024 * i : s1 - 1024 * i].bitcast(U32),
                 codes[a][:].bitcast(U32).indirect(offs_t[:, s0 // 16 : s1 // 16]),
             )
 
         def gather_bytes(s0, s1):
             nc.vector.tensor_copy(slot_planes[0][:, s0:s1], planes[:].indirect(offs_t[:, s0 // 16 : s1 // 16]))
             for a in (1, 2):
-                nc.scalar.dma_start(
-                    out=slot_planes[a][0:100, s0:s1].bitcast(I32),
-                    in_=slot_planes[0][4 * a : 4 * a + 100, s0:s1].bitcast(I32),
-                )
+                for q in range(4):
+                    nc.sync.dma_start(
+                        out=slot_planes[a][32 * q : 32 * q + 4, s0:s1].bitcast(I32),
+                        in_=slot_planes[0][32 * q + 4 * a : 32 * q + 4 * a + 4, s0:s1].bitcast(I32),
+                    )
 
         acc = {}
 
@@ -114,29 +118,30 @@ def tile_moe_tk_lin_relu2_kernel(
                     out=acc[(e, h)],
                     lhsT=w_t[:, e * A + a, :].bitcast(FP4X4),
                     lhsT_scale=ws_t[:, e * A + a, :],
-                    rhs=slot_codes[a][:, cols].bitcast(FP8X4),
+                    rhs=slot_codes[a][e // 4][:, (e % 4) * C + h * N : (e % 4) * C + h * N + N].bitcast(FP8X4),
                     rhs_scale=slot_planes[a][:, cols],
                     start=(a == 0),
                     stop=(a == A - 1),
                 )
 
-        def experts(es):
-            banks, rels = {}, {}
-            for e in es:
-                banks[e] = psum.tile([P, 512], F32, name="acc")
-                for h in range(2):
-                    acc[(e, h)] = banks[e][:, h * N : (h + 1) * N]
-                    multiply(e, h, (0, 1, 2))
+        def open_bank(e):
+            bank = psum.tile([P, 512], F32, name="acc")
+            for h in range(2):
+                acc[(e, h)] = bank[:, h * N : (h + 1) * N]
+            acc[e] = bank
+
+        def finish(es):
+            rels = {}
             for e in es:
                 rels[e] = ring.tile([P, C], F32, name="rel")
-                nc.scalar.activation(rels[e][:], banks[e][:, 0:C], ACT.Relu, bias=b_t[:, e : e + 1])
+                nc.scalar.activation(rels[e][:], acc[e][:, 0:C], ACT.Relu, bias=b_t[:, e : e + 1])
             for e in es:
                 nc.scalar.activation(y_t[:, e * C : (e + 1) * C], rels[e][:], ACT.Square)
 
         interleave(nc.vector.tensor_copy, 0, 0, 256)
-        interleave(nc.vector.tensor_copy, 0, 256, 384)
-        interleave(nc.scalar.copy, 0, 384, 512)
         quantise(0, 0, 256)
+        interleave(nc.scalar.copy, 0, 432, 512)
+        interleave(nc.vector.tensor_copy, 0, 256, 432)
         quantise(0, 256, 512)
         gather_words(0, 0, 1024)
         interleave(nc.scalar.copy, 1, 0, 512)
@@ -147,28 +152,51 @@ def tile_moe_tk_lin_relu2_kernel(
         quantise(2, 0, 512)
         gather_bytes(0, 1024)
         gather_bytes(1024, 2048)
-        gather_words(2, 0, 512)
-        experts((0, 1))
-        gather_words(2, 512, 1024)
-        experts((2, 3))
+        for e in range(4):
+            open_bank(e)
+            multiply(e, 0, (0,))
+        for e in range(4):
+            multiply(e, 0, (1,))
+        rel_pair = [keep.tile([P, 2 * C], F32, name=f"rel_pair{i}") for i in range(2)]
+        for i in range(2):
+            gather_words(2, 512 * i, 512 * i + 512)
+            for e in (2 * i, 2 * i + 1):
+                multiply(e, 0, (2,))
+                multiply(e, 1, (0, 1, 2))
+        for e in range(4):
+            nc.scalar.activation(
+                rel_pair[e // 2][:, (e % 2) * C : (e % 2 + 1) * C], acc[e][:, 0:C], ACT.Relu, bias=b_t[:, e : e + 1]
+            )
+            if e >= 2:
+                i = e - 2
+                nc.scalar.activation(y_t[:, 512 * i : 512 * i + 512], rel_pair[i][:], ACT.Square)
         gather_words(1, 1024, 1536)
+        for e in (4, 5):
+            open_bank(e)
+            multiply(e, 0, (0, 1))
         gather_words(2, 1024, 1536)
-        experts((4, 5))
+        for e in (4, 5):
+            multiply(e, 0, (2,))
+            multiply(e, 1, (0, 1, 2))
+        finish((4, 5))
         gather_words(1, 1536, 2048)
+        open_bank(6)
+        multiply(6, 0, (0, 1))
         for h in range(2):
             acc[(7, h)] = psum.tile([P, 512], F32, name="acc")[:, 0:N]
             multiply(7, h, (0, 1))
         gather_words(2, 1536, 1792)
-        experts((6,))
+        multiply(6, 0, (2,))
+        multiply(6, 1, (0, 1, 2))
+        finish((6,))
         gather_words(2, 1792, 2048)
-        last = 7 * C
-        rel7 = [keep.tile([P, N], F32, name=f"rel7_{h}") for h in range(2)]
         for h in range(2):
             multiply(7, h, (2,))
+        rel7 = [keep.tile([P, N], F32, name=f"rel7_{h}") for h in range(2)]
         for h in range(2):
             nc.vector.tensor_scalar(rel7[h][:], acc[(7, h)], b_t[:, 7:8], 0.0, ALU.add, ALU.max)
         for h in range(2):
-            nc.vector.tensor_tensor(y_t[:, last + h * N : last + (h + 1) * N], rel7[h][:], rel7[h][:], ALU.mult)
+            nc.vector.tensor_tensor(y_t[:, 7 * C + h * N : 7 * C + (h + 1) * N], rel7[h][:], rel7[h][:], ALU.mult)
 
         def fetch(r, t0, t1):
             nc.vector.tensor_tensor(
@@ -182,10 +210,10 @@ def tile_moe_tk_lin_relu2_kernel(
         fetch(1, 0, T)
         fetch(2, 0, T)
         nc.vector.tensor_tensor(sums[0][:], prod[0][:], prod[1][:], ALU.add)
-        fetch(3, 0, half)
-        nc.vector.tensor_tensor(sums[1][:], sums[0][:], prod[2][:], ALU.add)
-        fetch(3, half, T)
-        for t0 in (0, half):
-            cols = slice(t0, t0 + half)
+        fetch(3, 0, T)
+        halves = (slice(0, half), slice(half, T))
+        for cols in halves:
+            nc.vector.tensor_tensor(sums[1][:, cols], sums[0][:, cols], prod[2][:, cols], ALU.add)
+        for cols in halves:
             nc.vector.tensor_tensor(sums[2][:, cols], sums[1][:, cols], prod[3][:, cols], ALU.add)
-            (nc.sync if t0 == 0 else nc.scalar).dma_start(out=out[:, cols], in_=sums[2][:, cols])
+            nc.sync.dma_start(out=out[:, cols], in_=sums[2][:, cols])

from contextlib import ExitStack

import concourse.mybir as mybir

K, T, E, C, N = 1536, 512, 8, 256, 128
TOP = 4
SLOTS = E * C
P = 128
A = K // 512
FLOPS = 2 * K * N * SLOTS

F32 = mybir.dt.float32
BF16 = mybir.dt.bfloat16
I32 = mybir.dt.int32
U32 = mybir.dt.uint32
U16 = mybir.dt.uint16
U8 = mybir.dt.uint8
FP8X4 = mybir.dt.float8_e4m3fn_x4
FP4X4 = mybir.dt.float4_e2m1fn_x4
ACT = mybir.ActivationFunctionType
ALU = mybir.AluOpType


def tile_moe_tk_lin_relu2_kernel(
    tc, xT, w_words, w_scales, b, gate, offs, pos1, pos2, pos3, pos4, out
):
    nc = tc.nc
    with ExitStack() as ctx:
        keep = ctx.enter_context(tc.tile_pool(name="keep", bufs=1))
        ring = ctx.enter_context(tc.tile_pool(name="ring", bufs=3))
        psum = ctx.enter_context(tc.psum_pool(name="psum", bufs=8))

        offs_t = keep.tile([P, SLOTS // 16], U16, name="offs_t")
        pos_t = [keep.tile([P, T // 16], U16, name=f"pos_t{r}") for r in range(TOP)]
        x_raw = [keep.tile([P, 4, T], F32, name=f"x_raw{a}") for a in range(A)]
        x_bf = [keep.tile([P, T, 4], BF16, name=f"x_bf{a}", tag=f"share{a}", align_bytes=64) for a in range(A)]
        span = [1376, 1376, 704]
        codes = [keep.tile([P, span[a]], I32, name=f"codes{a}", align_bytes=64) for a in range(A)]
        planes = keep.tile([P, 1376], U8, name="planes", align_bytes=64)
        slot_codes = [[None, None], [None, None], [None, None]]
        slot_planes = [keep.tile([P, SLOTS], U8, name=f"slot_planes{a}", align_bytes=64) for a in range(A)]
        w_t = keep.tile([P, E * A, 2 * N], U8, name="w_t", align_bytes=64)
        ws_t = keep.tile([P, E * A, N], U8, name="ws_t", align_bytes=64)
        b_t = keep.tile([P, E], F32, name="b_t")
        gate_t = keep.tile([P, TOP, T], F32, name="gate_t")
        y_t = keep.tile([P, SLOTS], F32, name="y_t")
        prod = [keep.tile([P, T], F32, name=f"prod{r}") for r in range(TOP)]
        sums = [keep.tile([P, T], F32, name=f"sums{r}") for r in range(3)]
        warm = keep.tile([P, 2], F32, name="warm")

        def x_rows(a):
            return xT[a * 512 : (a + 1) * 512, :].rearrange("(p j) t -> p j t", j=4)

        half = T // 2
        nc.sync.dma_start(out=x_raw[0][:, :, 0:half], in_=x_rows(0)[:, :, 0:half])
        nc.sync.dma_start(out=x_raw[0][:, :, half:T], in_=x_rows(0)[:, :, half:T])
        nc.sync.dma_start(offs_t[:], offs)
        nc.sync.dma_start(out=x_raw[1][:], in_=x_rows(1))
        nc.sync.dma_start(out=x_raw[2][:], in_=x_rows(2))

        w_rows = w_words.rearrange("e a p c -> p (e a) c")
        ws_rows = w_scales.rearrange("e a q n -> q (e a) n")
        nc.gpsimd.memset(ws_t[:].rearrange("p i n -> p (i n)").bitcast(I32), 0)
        nc.sync.dma_start(out=w_t[:].bitcast(I32), in_=w_rows.bitcast(I32))
        for q in range(4):
            nc.sync.dma_start(
                out=ws_t[32 * q : 32 * q + 4, :, :].bitcast(I32),
                in_=ws_rows[4 * q : 4 * q + 4, :, :].bitcast(I32),
            )
        nc.sync.dma_start(out=b_t[:], in_=b)
        for r, pos in enumerate((pos1, pos2, pos3, pos4)):
            nc.sync.dma_start(pos_t[r][:], pos)
        nc.sync.dma_start(out=gate_t[:], in_=gate.rearrange("r p t -> p r t"))

        nc.vector.memset(warm[:, 0:1], 0.0)
        nc.scalar.activation(warm[:, 1:2], warm[:, 0:1], ACT.Relu)
        nc.vector.memset(planes[:].bitcast(I32), 0)
        for a in range(A):
            nc.vector.memset(codes[a][:, T:], 0)
        for a in (1, 2):
            nc.gpsimd.memset(slot_planes[a][:].bitcast(I32), 0)

        def interleave(copy, a, t0, t1):
            copy(x_bf[a][:, t0:t1, :], x_raw[a][:, :, t0:t1].rearrange("p j t -> p t j"))

        def quantise(a, t0, t1):
            nc.vector.quantize_mx(
                out=codes[a][:, t0:t1].bitcast(FP8X4),
                scales=planes[4 * a : P, t0:t1],
                in_=x_bf[a][:, t0:t1, :].rearrange("p t j -> p (t j)"),
            )

        def gather_words(a, s0, s1):
            i = s0 // 1024
            if slot_codes[a][i] is None:
                tag = "share2" if (a, i) == (1, 1) else f"slot_codes{a}_{i}"
                slot_codes[a][i] = keep.tile([P, 1024], I32, name=f"slot_codes{a}_{i}", tag=tag, align_bytes=64)
            nc.vector.tensor_copy(
                slot_codes[a][i][:, s0 - 1024 * i : s1 - 1024 * i].bitcast(U32),
                codes[a][:].bitcast(U32).indirect(offs_t[:, s0 // 16 : s1 // 16]),
            )

        def gather_bytes(s0, s1):
            nc.vector.tensor_copy(slot_planes[0][:, s0:s1], planes[:].indirect(offs_t[:, s0 // 16 : s1 // 16]))
            for a in (1, 2):
                for q in range(4):
                    nc.sync.dma_start(
                        out=slot_planes[a][32 * q : 32 * q + 4, s0:s1].bitcast(I32),
                        in_=slot_planes[0][32 * q + 4 * a : 32 * q + 4 * a + 4, s0:s1].bitcast(I32),
                    )

        acc = {}

        def multiply(e, h, passes):
            cols = slice(e * C + h * N, e * C + h * N + N)
            for a in passes:
                nc.tensor.matmul_mx(
                    out=acc[(e, h)],
                    lhsT=w_t[:, e * A + a, :].bitcast(FP4X4),
                    lhsT_scale=ws_t[:, e * A + a, :],
                    rhs=slot_codes[a][e // 4][:, (e % 4) * C + h * N : (e % 4) * C + h * N + N].bitcast(FP8X4),
                    rhs_scale=slot_planes[a][:, cols],
                    start=(a == 0),
                    stop=(a == A - 1),
                )

        def open_bank(e):
            bank = psum.tile([P, 512], F32, name="acc")
            for h in range(2):
                acc[(e, h)] = bank[:, h * N : (h + 1) * N]
            acc[e] = bank

        def finish(es):
            rels = {}
            for e in es:
                rels[e] = ring.tile([P, C], F32, name="rel")
                nc.scalar.activation(rels[e][:], acc[e][:, 0:C], ACT.Relu, bias=b_t[:, e : e + 1])
            for e in es:
                nc.scalar.activation(y_t[:, e * C : (e + 1) * C], rels[e][:], ACT.Square)

        interleave(nc.vector.tensor_copy, 0, 0, 256)
        quantise(0, 0, 256)
        interleave(nc.scalar.copy, 0, 432, 512)
        interleave(nc.vector.tensor_copy, 0, 256, 432)
        quantise(0, 256, 512)
        gather_words(0, 0, 1024)
        interleave(nc.scalar.copy, 1, 0, 512)
        gather_words(0, 1024, 2048)
        quantise(1, 0, 512)
        interleave(nc.scalar.copy, 2, 0, 512)
        gather_words(1, 0, 1024)
        quantise(2, 0, 512)
        gather_bytes(0, 1024)
        gather_bytes(1024, 2048)
        for e in range(4):
            open_bank(e)
            multiply(e, 0, (0,))
        for e in range(4):
            multiply(e, 0, (1,))
        rel_pair = [keep.tile([P, 2 * C], F32, name=f"rel_pair{i}") for i in range(2)]
        for i in range(2):
            gather_words(2, 512 * i, 512 * i + 512)
            for e in (2 * i, 2 * i + 1):
                multiply(e, 0, (2,))
                multiply(e, 1, (0, 1, 2))
        for e in range(4):
            nc.scalar.activation(
                rel_pair[e // 2][:, (e % 2) * C : (e % 2 + 1) * C], acc[e][:, 0:C], ACT.Relu, bias=b_t[:, e : e + 1]
            )
            if e >= 2:
                i = e - 2
                nc.scalar.activation(y_t[:, 512 * i : 512 * i + 512], rel_pair[i][:], ACT.Square)
        gather_words(1, 1024, 1536)
        for e in (4, 5):
            open_bank(e)
            multiply(e, 0, (0, 1))
        gather_words(2, 1024, 1536)
        for e in (4, 5):
            multiply(e, 0, (2,))
            multiply(e, 1, (0, 1, 2))
        finish((4, 5))
        gather_words(1, 1536, 2048)
        open_bank(6)
        multiply(6, 0, (0, 1))
        for h in range(2):
            acc[(7, h)] = psum.tile([P, 512], F32, name="acc")[:, 0:N]
            multiply(7, h, (0, 1))
        gather_words(2, 1536, 1792)
        multiply(6, 0, (2,))
        multiply(6, 1, (0, 1, 2))
        finish((6,))
        gather_words(2, 1792, 2048)
        for h in range(2):
            multiply(7, h, (2,))
        rel7 = [keep.tile([P, N], F32, name=f"rel7_{h}") for h in range(2)]
        for h in range(2):
            nc.vector.tensor_scalar(rel7[h][:], acc[(7, h)], b_t[:, 7:8], 0.0, ALU.add, ALU.max)
        for h in range(2):
            nc.vector.tensor_tensor(y_t[:, 7 * C + h * N : 7 * C + (h + 1) * N], rel7[h][:], rel7[h][:], ALU.mult)

        def fetch(r, t0, t1):
            nc.vector.tensor_tensor(
                prod[r][:, t0:t1],
                y_t[:].indirect(pos_t[r][:, t0 // 16 : t1 // 16]),
                gate_t[:, r, t0:t1],
                ALU.mult,
            )

        fetch(0, 0, T)
        fetch(1, 0, T)
        fetch(2, 0, T)
        nc.vector.tensor_tensor(sums[0][:], prod[0][:], prod[1][:], ALU.add)
        fetch(3, 0, T)
        halves = (slice(0, half), slice(half, T))
        for cols in halves:
            nc.vector.tensor_tensor(sums[1][:, cols], sums[0][:, cols], prod[2][:, cols], ALU.add)
        for cols in halves:
            nc.vector.tensor_tensor(sums[2][:, cols], sums[1][:, cols], prod[3][:, cols], ALU.add)
            nc.sync.dma_start(out=out[:, cols], in_=sums[2][:, cols])
